import numpy as np
import ml_dtypes


def mxq(x, axis, fmt="e4m3"):
    dtype, down = {"e4m3": (ml_dtypes.float8_e4m3fn, 7), "e5m2": (ml_dtypes.float8_e5m2, 14)}[fmt]
    v = np.moveaxis(np.asarray(x, np.float32).astype(ml_dtypes.bfloat16).astype(np.float64), axis, -1)
    blocks = v.reshape(v.shape[:-1] + (-1, 32))
    amax = np.abs(blocks).max(-1, keepdims=True)
    byte = np.maximum(np.where(amax > 0, np.frexp(amax)[1] - 1 + 127, 0) - down, 1)
    scale = np.exp2(byte - 127.0)
    codes = (blocks / scale).astype(np.float32).astype(dtype).astype(np.float64)
    return np.moveaxis((codes * scale).reshape(v.shape), -1, axis)


WIDE = False


def mx_kscale(k):
    if not WIDE:
        return np.ones(k)
    levels = np.array([30, -30])
    if k % 512:
        return np.exp2(np.random.permutation(np.resize(levels, k // 32))).repeat(32)
    a = np.empty((k // 512, 16))
    for p in range(k // 512):
        a[p, :8] = np.random.permutation(np.resize(levels, 8))
        for g in range(8):
            far = levels[np.abs(levels - a[p, g]) >= 10]
            a[p, g + 8] = far[np.random.randint(len(far))]
    return np.exp2(a.ravel()).repeat(32)


def f64(x):
    return np.asarray(x).astype(np.float64)


def striped(idx):
    return np.tile(np.asarray(idx).reshape(-1, 16).T, (8, 1)).astype(np.uint16)


def unstriped(offs):
    return offs[:16].T.reshape(-1).astype(np.int64)


E2M1 = np.array([0.0, 0.5, 1.0, 1.5, 2.0, 3.0, 4.0, 6.0, -0.0, -0.5, -1.0, -1.5, -2.0, -3.0, -4.0, -6.0])


def pack_weight(w, fmt):
    k, n = w.shape
    w = f64(np.asarray(w, np.float32).astype(ml_dtypes.bfloat16)).reshape(k // 32, 32, n)
    amax = np.abs(w).max(1)
    if fmt in ("e4m3", "e5m2"):
        byte = np.frexp(amax)[1] - 1 + 127 - (7 if fmt == "e4m3" else 14)
    else:
        mant, ex = np.frexp(amax / 6.0)
        byte = np.where(mant > 0.5, ex, ex - 1) + 127
    byte = np.clip(np.where(amax > 0, byte, 1), 1, 254)
    scaled = (w * np.exp2(127.0 - byte)[:, None, :]).reshape(k, n).astype(np.float32)
    by_word = np.ascontiguousarray(scaled.reshape(k // 512, 128, 4, n).transpose(0, 1, 3, 2))
    if fmt in ("e4m3", "e5m2"):
        words = by_word.astype(ml_dtypes.float8_e4m3fn if fmt == "e4m3" else ml_dtypes.float8_e5m2).view(np.uint8)
    else:
        c = by_word.astype(ml_dtypes.float4_e2m1fn).view(np.uint8) & 0xF
        words = (c[..., 0::2] | (c[..., 1::2] << 4)).reshape(k // 512, 128, 2 * n)
    return np.ascontiguousarray(words), np.ascontiguousarray(byte.astype(np.uint8).reshape(k // 512, 16, n))


def unpack_weight(words, scales, fmt):
    g, _, n = scales.shape
    words = np.ascontiguousarray(words).reshape(g, 128, n, -1)
    if fmt in ("e4m3", "e5m2"):
        vals = words.view(ml_dtypes.float8_e4m3fn if fmt == "e4m3" else ml_dtypes.float8_e5m2).astype(np.float64)
    else:
        nib = np.empty((g, 128, n, 4), np.uint8)
        nib[..., 0::2] = words & 0xF
        nib[..., 1::2] = words >> 4
        vals = E2M1[nib]
    vals = vals * np.repeat(np.exp2(scales.astype(np.float64) - 127.0), 8, axis=1)[..., None]
    return vals.transpose(0, 1, 3, 2).reshape(g * 512, n)


K, T, J, R, C, D, O, N, S = 512, 2048, 256, 512, 512, 512, 256, 256, 1024


def setup_inputs():
    n = np.random.standard_normal
    idx = np.random.permutation(T)[:J]
    idx2 = np.random.permutation(T)[:J]
    idx3 = np.random.permutation(C)[:J]
    idx4 = np.random.permutation(D)[:J]
    idx5 = np.random.permutation(C)[:O]
    idx6 = np.random.permutation(D)[:O]
    idx7 = np.random.permutation(S)[:N]
    fk = mx_kscale(K)
    fr = mx_kscale(R)
    xtp = pack_weight(n((K, T)) / fk[:, None], "e2m1")
    wp = pack_weight(n((K, R)) * 1 / np.sqrt(K) * fk[:, None] * fr, "e5m2")
    vsp = pack_weight(n((R, S)) * 1 / np.sqrt(R) / fr[:, None], "e4m3")
    return {
        "xt_words": xtp[0],
        "xt_scales": xtp[1],
        "w_words": wp[0],
        "w_scales": wp[1],
        "sa": (np.random.uniform(0.5, 1.6, (R, 1))).astype(np.float32),
        "sb": (np.random.uniform(0.5, 1.6, (R, 1))).astype(np.float32),
        "vs_words": vsp[0],
        "vs_scales": vsp[1],
        "offs": striped(idx),
        "offs2": striped(idx2),
        "offs3": striped(idx3),
        "offs4": striped(idx4),
        "offs5": striped(idx5),
        "offs6": striped(idx6),
        "offs7": striped(idx7),
    }


def reference(xt_words, xt_scales, w_words, w_scales, sa, sb, vs_words, vs_scales, offs, offs2, offs3, offs4, offs5, offs6, offs7):
    idx = unstriped(offs)
    idx2 = unstriped(offs2)
    idx3 = unstriped(offs3)
    idx4 = unstriped(offs4)
    idx5 = unstriped(offs5)
    idx6 = unstriped(offs6)
    idx7 = unstriped(offs7)
    xtu = unpack_weight(xt_words, xt_scales, "e2m1")
    wu = unpack_weight(w_words, w_scales, "e5m2")
    vsu = unpack_weight(vs_words, vs_scales, "e4m3")
    xtidxg = xtu[:, idx]
    a = wu.T @ xtidxg
    xtidx2g = xtu[:, idx2]
    b = wu.T @ xtidx2g
    pw = np.zeros((R, C))
    pw[:, idx3] = a
    pv = np.zeros((R, D))
    pv[:, idx4] = b
    hid = np.abs(pw[:, idx5] * f64(sa) - pv[:, idx6] * f64(sb))
    vsidx7g = vsu[:, idx7]
    hidq = mxq(hid, 0, "e5m2")
    y = vsidx7g.T @ hidq
    return y

@@ -1,0 +1,174 @@
+from contextlib import ExitStack
+
+import concourse.mybir as mybir
+
+K, T, J, R, C, O, N, S = 512, 2048, 256, 512, 512, 256, 256, 1024
+FLOPS = 2 * (2 * K * R * J + R * N * O)
+
+F32 = mybir.dt.float32
+BF16 = mybir.dt.bfloat16
+I32 = mybir.dt.int32
+U32 = mybir.dt.uint32
+U16 = mybir.dt.uint16
+U8 = mybir.dt.uint8
+E2M1 = mybir.dt.float4_e2m1fn_x4
+E5M2 = mybir.dt.float8_e5m2_x4
+E4M3 = mybir.dt.float8_e4m3fn_x4
+ALU = mybir.AluOpType
+ACT = mybir.ActivationFunctionType
+
+P = 128
+PACK = 4
+QUADS = 4
+QROWS = 4
+HALF = O // 2
+
+
+def tile_list_twoboardsweighed_tied_store_plain_kernel(
+    tc, xt_words, xt_scales, w_words, w_scales, sa, sb, vs_words, vs_scales,
+    offs, offs2, offs3, offs4, offs5, offs6, offs7, out,
+):
+    nc = tc.nc
+    with ExitStack() as ctx:
+        keep = ctx.enter_context(tc.tile_pool(name="keep", bufs=1))
+        psum = ctx.enter_context(tc.psum_pool(name="psum", bufs=1))
+
+        def tile(shape, dtype, name):
+            return keep.tile(shape, dtype, name=name, align_bytes=64)
+
+        def load_list(src, name):
+            dst = tile([P, J // 16], U16, name)
+            nc.sync.dma_start(dst[:], src)
+            return dst
+
+        def load_plane(dst, src):
+            for q in range(QUADS):
+                nc.sync.dma_start(
+                    dst[32 * q : 32 * q + QROWS, :].bitcast(I32),
+                    src[0, QROWS * q : QROWS * (q + 1), :].bitcast(I32),
+                )
+
+        xs = tile([P, T], U8, "xs")
+        ws = tile([P, R], U8, "ws")
+        vsc = tile([P, S], U8, "vsc")
+        nc.vector.memset(xs[:].bitcast(I32), 0)
+        nc.vector.memset(ws[:].bitcast(I32), 0)
+        pw = [tile([P, C], F32, f"pw{t}") for t in range(PACK)]
+        pv = [tile([P, C], F32, f"pv{t}") for t in range(PACK)]
+        nc.gpsimd.memset(vsc[:].bitcast(I32), 0)
+        for t in range(PACK):
+            nc.gpsimd.memset(pw[t][:], 0.0)
+            nc.gpsimd.memset(pv[t][:], 0.0)
+
+        l1 = load_list(offs, "l1")
+        xw = tile([P, T], U16, "xw")
+        nc.sync.dma_start(xw[:].bitcast(I32), xt_words[0].bitcast(I32))
+        ws_rows = tile([QROWS, QUADS, R // 4], I32, "ws_rows")
+        nc.scalar.dma_start(ws_rows[:], w_scales[0].bitcast(I32).rearrange("(q r) c -> r q c", r=QROWS))
+        ww = tile([P, R], U32, "ww")
+        nc.scalar.dma_start(ww[:].bitcast(I32), w_words[0].rearrange("p c b -> p (c b)").bitcast(I32))
+        load_plane(xs, xt_scales)
+        l2 = load_list(offs2, "l2")
+        l3 = load_list(offs3, "l3")
+        l4 = load_list(offs4, "l4")
+        l5 = load_list(offs5, "l5")
+        l6 = load_list(offs6, "l6")
+        sa_sb = tile([P, PACK], F32, "sa_sb")
+        sb_sb = tile([P, PACK], F32, "sb_sb")
+        nc.sync.dma_start(sa_sb[:], sa.rearrange("(p t) one -> p (t one)", t=PACK))
+        nc.sync.dma_start(sb_sb[:], sb.rearrange("(p t) one -> p (t one)", t=PACK))
+        l7 = load_list(offs7, "l7")
+        vw = tile([P, S], U32, "vw")
+        nc.sync.dma_start(vw[:].bitcast(I32), vs_words[0].rearrange("p c b -> p (c b)").bitcast(I32))
+        load_plane(vsc, vs_scales)
+
+        for q in range(QUADS):
+            nc.vector.tensor_copy(ws[32 * q : 32 * q + QROWS, :].bitcast(I32), ws_rows[:, q, :])
+        wsp = tile([P, R], U8, "wsp")
+        nc.vector.tensor_copy(
+            wsp[:].rearrange("p (t c i) -> p c t i", t=PACK, i=16),
+            ws[:].rearrange("p (c i t) -> p c t i", t=PACK, i=16),
+        )
+        wwp = tile([P, R], U32, "wwp")
+        nc.scalar.copy(
+            wwp[:].rearrange("p (t c i) -> p c t i", t=PACK, i=4),
+            ww[:].rearrange("p (c i t) -> p c t i", t=PACK, i=4),
+        )
+
+        sums = []
+        for name, lst in (("a", l1), ("b", l2)):
+            gs = tile([P, J], U8, f"gs_{name}")
+            gw = tile([P, J], U16, f"gw_{name}")
+            nc.vector.tensor_copy(gs[:], xs[:].indirect(lst[:]))
+            nc.vector.tensor_copy(gw[:], xw[:].indirect(lst[:]))
+            banks = []
+            for h in range(2):
+                bank = psum.tile([P, 2, J], F32, name=f"ps_{name}{h}")
+                for u in range(2):
+                    cols = slice(P * (2 * h + u), P * (2 * h + u + 1))
+                    nc.tensor.matmul_mx(
+                        bank[:, u, :],
+                        lhsT=wwp[:, cols].bitcast(E5M2), lhsT_scale=wsp[:, cols],
+                        rhs=gw[:].bitcast(E2M1), rhs_scale=gs[:],
+                        start=True, stop=True,
+                    )
+                banks.append(bank)
+            sums.append(banks)
+
+        a_sb = [tile([P, 2, J], F32, f"a_sb{h}") for h in range(2)]
+        b_sb = [tile([P, 2, J], F32, f"b_sb{h}") for h in range(2)]
+        nc.scalar.copy(a_sb[0][:], sums[0][0][:])
+        nc.scalar.copy(a_sb[1][:], sums[0][1][:])
+        nc.scalar.copy(b_sb[0][:], sums[1][0][:])
+        nc.vector.tensor_copy(pw[0][:].indirect(l3[:]), a_sb[0][:, 0, :])
+        nc.vector.tensor_copy(b_sb[1][:], sums[1][1][:])
+        for t in range(1, PACK):
+            nc.vector.tensor_copy(pw[t][:].indirect(l3[:]), a_sb[t // 2][:, t % 2, :])
+        for t in range(PACK - 1):
+            nc.scalar.activation(pv[t][:].indirect(l4[:]), b_sb[t // 2][:, t % 2, :], ACT.Copy)
+        nc.vector.tensor_copy(pv[3][:].indirect(l4[:]), b_sb[1][:, 1, :])
+
+        vgs = tile([P, N], U8, "vgs")
+        vgw = tile([P, N], U32, "vgw")
+        nc.vector.tensor_copy(vgw[:], vw[:].indirect(l7[:]))
+        nc.vector.tensor_copy(vgs[:], vsc[:].indirect(l7[:]))
+
+        diff = tile([P, PACK, O], F32, "diff")
+        for t in range(PACK):
+            ua = tile([P, O], F32, f"ua{t}")
+            ub = tile([P, O], F32, f"ub{t}")
+            nc.scalar.activation(ua[:], pw[t][:].indirect(l5[:]), ACT.Copy, scale=sa_sb[:, t : t + 1])
+            nc.scalar.activation(ub[:], pv[t][:].indirect(l6[:]), ACT.Copy, scale=sb_sb[:, t : t + 1])
+            nc.vector.tensor_tensor(diff[:, t, :], ua[:], ub[:], ALU.subtract)
+
+        hq = tile([P, O], U32, "hq")
+        hs = tile([P, O], U8, "hs")
+        hid0 = tile([P, HALF, PACK], BF16, "hid0")
+        hid1 = tile([P, HALF, PACK], BF16, "hid1")
+        d0 = diff[:, :, 0:HALF].rearrange("p t o -> p o t")
+        nc.vector.scalar_tensor_tensor(hid0[:], d0, -1.0, d0, ALU.mult, ALU.max)
+        nc.scalar.activation(
+            hid1[:].rearrange("p (c i) t -> p c t i", i=4),
+            diff[:, :, HALF:O].rearrange("p t (c i) -> p c t i", i=4),
+            ACT.Abs,
+        )
+        for h, hid in enumerate((hid0, hid1)):
+            cols = slice(HALF * h, HALF * (h + 1))
+            nc.vector.quantize_mx(hq[:, cols].bitcast(E5M2), hs[:, cols], hid[:].rearrange("p o t -> p (o t)"))
+
+        for h in range(2):
+            rows = slice(P * h, P * (h + 1))
+            y = psum.tile([P, O], F32, name=f"ps_y{h}")
+            nc.tensor.matmul_mx(
+                y[:],
+                lhsT=vgw[:, rows].bitcast(E4M3), lhsT_scale=vgs[:, rows],
+                rhs=hq[:].bitcast(E5M2), rhs_scale=hs[:],
+                start=True, stop=True,
+            )
+            y_sb = tile([P, O], F32, f"y_sb{h}")
+            if h == 0:
+                nc.scalar.copy(y_sb[:], y[:])
+                nc.scalar.dma_start(out[rows, :], y_sb[:])
+            else:
+                nc.vector.tensor_copy(y_sb[:], y[:])
+                nc.sync.dma_start(out[rows, :], y_sb[:])

@@ -21,7 +21,7 @@ P = 128
 PACK = 4
 QUADS = 4
 QROWS = 4
-HALF = O // 2
+SPLIT = 112
 
 
 def tile_list_twoboardsweighed_tied_store_plain_kernel(
@@ -33,8 +33,8 @@ def tile_list_twoboardsweighed_tied_store_plain_kernel(
         keep = ctx.enter_context(tc.tile_pool(name="keep", bufs=1))
         psum = ctx.enter_context(tc.psum_pool(name="psum", bufs=1))
 
-        def tile(shape, dtype, name):
-            return keep.tile(shape, dtype, name=name, align_bytes=64)
+        def tile(shape, dtype, name, tag=None):
+            return keep.tile(shape, dtype, name=name, tag=tag or name, align_bytes=64)
 
         def load_list(src, name):
             dst = tile([P, J // 16], U16, name)
@@ -53,21 +53,19 @@ def tile_list_twoboardsweighed_tied_store_plain_kernel(
         vsc = tile([P, S], U8, "vsc")
         nc.vector.memset(xs[:].bitcast(I32), 0)
         nc.vector.memset(ws[:].bitcast(I32), 0)
-        pw = [tile([P, C], F32, f"pw{t}") for t in range(PACK)]
-        pv = [tile([P, C], F32, f"pv{t}") for t in range(PACK)]
-        nc.gpsimd.memset(vsc[:].bitcast(I32), 0)
-        for t in range(PACK):
-            nc.gpsimd.memset(pw[t][:], 0.0)
-            nc.gpsimd.memset(pv[t][:], 0.0)
+        pw = [tile([P, C], F32, f"pw{t}") for t in range(2)]
+        for t in range(2):
+            nc.vector.memset(pw[t][:], 0.0)
+        nc.vector.memset(vsc[:].bitcast(I32), 0)
 
         l1 = load_list(offs, "l1")
         xw = tile([P, T], U16, "xw")
         nc.sync.dma_start(xw[:].bitcast(I32), xt_words[0].bitcast(I32))
         ws_rows = tile([QROWS, QUADS, R // 4], I32, "ws_rows")
         nc.scalar.dma_start(ws_rows[:], w_scales[0].bitcast(I32).rearrange("(q r) c -> r q c", r=QROWS))
-        ww = tile([P, R], U32, "ww")
-        nc.scalar.dma_start(ww[:].bitcast(I32), w_words[0].rearrange("p c b -> p (c b)").bitcast(I32))
         load_plane(xs, xt_scales)
+        ww = tile([P, R], U32, "ww")
+        nc.sync.dma_start(ww[:].bitcast(I32), w_words[0].rearrange("p c b -> p (c b)").bitcast(I32))
         l2 = load_list(offs2, "l2")
         l3 = load_list(offs3, "l3")
         l4 = load_list(offs4, "l4")
@@ -95,17 +93,16 @@ def tile_list_twoboardsweighed_tied_store_plain_kernel(
             ww[:].rearrange("p (c i t) -> p c t i", t=PACK, i=4),
         )
 
-        sums = []
-        for name, lst in (("a", l1), ("b", l2)):
-            gs = tile([P, J], U8, f"gs_{name}")
+        def first_stage(name, lst, groups):
             gw = tile([P, J], U16, f"gw_{name}")
-            nc.vector.tensor_copy(gs[:], xs[:].indirect(lst[:]))
+            gs = tile([P, J], U8, f"gs_{name}")
             nc.vector.tensor_copy(gw[:], xw[:].indirect(lst[:]))
+            nc.vector.tensor_copy(gs[:], xs[:].indirect(lst[:]))
             banks = []
-            for h in range(2):
-                bank = psum.tile([P, 2, J], F32, name=f"ps_{name}{h}")
-                for u in range(2):
-                    cols = slice(P * (2 * h + u), P * (2 * h + u + 1))
+            for group in groups:
+                bank = psum.tile([P, len(group), J], F32, name=f"ps_{name}{group[0]}")
+                for u, t in enumerate(group):
+                    cols = slice(P * t, P * (t + 1))
                     nc.tensor.matmul_mx(
                         bank[:, u, :],
                         lhsT=wwp[:, cols].bitcast(E5M2), lhsT_scale=wsp[:, cols],
@@ -113,20 +110,36 @@ def tile_list_twoboardsweighed_tied_store_plain_kernel(
                         start=True, stop=True,
                     )
                 banks.append(bank)
-            sums.append(banks)
+            return banks
 
-        a_sb = [tile([P, 2, J], F32, f"a_sb{h}") for h in range(2)]
-        b_sb = [tile([P, 2, J], F32, f"b_sb{h}") for h in range(2)]
-        nc.scalar.copy(a_sb[0][:], sums[0][0][:])
-        nc.scalar.copy(a_sb[1][:], sums[0][1][:])
-        nc.scalar.copy(b_sb[0][:], sums[1][0][:])
-        nc.vector.tensor_copy(pw[0][:].indirect(l3[:]), a_sb[0][:, 0, :])
-        nc.vector.tensor_copy(b_sb[1][:], sums[1][1][:])
-        for t in range(1, PACK):
-            nc.vector.tensor_copy(pw[t][:].indirect(l3[:]), a_sb[t // 2][:, t % 2, :])
-        for t in range(PACK - 1):
-            nc.scalar.activation(pv[t][:].indirect(l4[:]), b_sb[t // 2][:, t % 2, :], ACT.Copy)
-        nc.vector.tensor_copy(pv[3][:].indirect(l4[:]), b_sb[1][:, 1, :])
+        ps_a = first_stage("a", l1, ((0,), (1,), (2, 3)))
+        ps_b = first_stage("b", l2, ((0, 1), (2, 3)))
+
+        def late_page(name, tag):
+            page = tile([P, C], F32, name, tag)
+            nc.gpsimd.memset(page[:], 0.0)
+            return page
+
+        pw.extend([late_page("pw2", "ws"), late_page("pw3", "ww")])
+        pv = [late_page(f"pv{t}", tag) for t, tag in enumerate(("xw", "xs", "gw_a", "gs_a"))]
+
+        a0 = tile([P, 1, J], F32, "a0")
+        a1 = tile([P, 1, J], F32, "a1")
+        a23 = tile([P, 2, J], F32, "a23")
+        b01 = tile([P, 2, J], F32, "b01")
+        b23 = tile([P, 2, J], F32, "b23")
+        nc.scalar.copy(a0[:], ps_a[0][:])
+        nc.scalar.copy(a1[:], ps_a[1][:])
+        nc.vector.tensor_copy(pw[0][:].indirect(l3[:]), a0[:, 0, :])
+        nc.scalar.activation(pw[1][:].indirect(l3[:]), a1[:, 0, :], ACT.Copy)
+        nc.vector.tensor_copy(a23[:], ps_a[2][:])
+        nc.scalar.copy(b01[:], ps_b[0][:])
+        nc.scalar.copy(b23[:], ps_b[1][:])
+        for u in range(2):
+            nc.vector.tensor_copy(pw[2 + u][:].indirect(l3[:]), a23[:, u, :])
+            nc.scalar.activation(pv[u][:].indirect(l4[:]), b01[:, u, :], ACT.Copy)
+        for u in range(2):
+            nc.vector.tensor_copy(pv[2 + u][:].indirect(l4[:]), b23[:, u, :])
 
         vgs = tile([P, N], U8, "vgs")
         vgw = tile([P, N], U32, "vgw")
@@ -143,18 +156,15 @@ def tile_list_twoboardsweighed_tied_store_plain_kernel(
 
         hq = tile([P, O], U32, "hq")
         hs = tile([P, O], U8, "hs")
-        hid0 = tile([P, HALF, PACK], BF16, "hid0")
-        hid1 = tile([P, HALF, PACK], BF16, "hid1")
-        d0 = diff[:, :, 0:HALF].rearrange("p t o -> p o t")
-        nc.vector.scalar_tensor_tensor(hid0[:], d0, -1.0, d0, ALU.mult, ALU.max)
+        hid = tile([P, O, PACK], BF16, "hid")
+        d0 = diff[:, :, 0:SPLIT].rearrange("p t o -> p o t")
+        nc.vector.scalar_tensor_tensor(hid[:, 0:SPLIT, :], d0, -1.0, d0, ALU.mult, ALU.max)
         nc.scalar.activation(
-            hid1[:].rearrange("p (c i) t -> p c t i", i=4),
-            diff[:, :, HALF:O].rearrange("p t (c i) -> p c t i", i=4),
+            hid[:, SPLIT:O, :].rearrange("p (c i) t -> p c t i", i=4),
+            diff[:, :, SPLIT:O].rearrange("p t (c i) -> p c t i", i=4),
             ACT.Abs,
         )
-        for h, hid in enumerate((hid0, hid1)):
-            cols = slice(HALF * h, HALF * (h + 1))
-            nc.vector.quantize_mx(hq[:, cols].bitcast(E5M2), hs[:, cols], hid[:].rearrange("p o t -> p (o t)"))
+        nc.vector.quantize_mx(hq[:].bitcast(E5M2), hs[:], hid[:].rearrange("p o t -> p (o t)"))
 
         for h in range(2):
             rows = slice(P * h, P * (h + 1))

@@ -21,7 +21,8 @@ P = 128
 PACK = 4
 QUADS = 4
 QROWS = 4
-SPLIT = 112
+HALF = O // 2
+CUT = 168
 
 
 def tile_list_twoboardsweighed_tied_store_plain_kernel(
@@ -68,6 +69,10 @@ def tile_list_twoboardsweighed_tied_store_plain_kernel(
         nc.sync.dma_start(ww[:].bitcast(I32), w_words[0].rearrange("p c b -> p (c b)").bitcast(I32))
         l2 = load_list(offs2, "l2")
         l3 = load_list(offs3, "l3")
+        l7 = load_list(offs7, "l7")
+        vw = tile([P, S], U32, "vw")
+        nc.sync.dma_start(vw[:].bitcast(I32), vs_words[0].rearrange("p c b -> p (c b)").bitcast(I32))
+        load_plane(vsc, vs_scales)
         l4 = load_list(offs4, "l4")
         l5 = load_list(offs5, "l5")
         l6 = load_list(offs6, "l6")
@@ -75,10 +80,6 @@ def tile_list_twoboardsweighed_tied_store_plain_kernel(
         sb_sb = tile([P, PACK], F32, "sb_sb")
         nc.sync.dma_start(sa_sb[:], sa.rearrange("(p t) one -> p (t one)", t=PACK))
         nc.sync.dma_start(sb_sb[:], sb.rearrange("(p t) one -> p (t one)", t=PACK))
-        l7 = load_list(offs7, "l7")
-        vw = tile([P, S], U32, "vw")
-        nc.sync.dma_start(vw[:].bitcast(I32), vs_words[0].rearrange("p c b -> p (c b)").bitcast(I32))
-        load_plane(vsc, vs_scales)
 
         for q in range(QUADS):
             nc.vector.tensor_copy(ws[32 * q : 32 * q + QROWS, :].bitcast(I32), ws_rows[:, q, :])
@@ -88,10 +89,11 @@ def tile_list_twoboardsweighed_tied_store_plain_kernel(
             ws[:].rearrange("p (c i t) -> p c t i", t=PACK, i=16),
         )
         wwp = tile([P, R], U32, "wwp")
-        nc.scalar.copy(
-            wwp[:].rearrange("p (t c i) -> p c t i", t=PACK, i=4),
-            ww[:].rearrange("p (c i t) -> p c t i", t=PACK, i=4),
-        )
+        for t0 in (0, 2):
+            nc.scalar.copy(
+                wwp[:].rearrange("p (t c i) -> p c t i", t=PACK, i=4)[:, :, t0 : t0 + 2, :],
+                ww[:].rearrange("p (c i t) -> p c t i", t=PACK, i=4)[:, :, t0 : t0 + 2, :],
+            )
 
         def first_stage(name, lst, groups):
             gw = tile([P, J], U16, f"gw_{name}")
@@ -134,10 +136,10 @@ def tile_list_twoboardsweighed_tied_store_plain_kernel(
         nc.scalar.activation(pw[1][:].indirect(l3[:]), a1[:, 0, :], ACT.Copy)
         nc.vector.tensor_copy(a23[:], ps_a[2][:])
         nc.scalar.copy(b01[:], ps_b[0][:])
-        nc.scalar.copy(b23[:], ps_b[1][:])
         for u in range(2):
             nc.vector.tensor_copy(pw[2 + u][:].indirect(l3[:]), a23[:, u, :])
             nc.scalar.activation(pv[u][:].indirect(l4[:]), b01[:, u, :], ACT.Copy)
+        nc.vector.tensor_copy(b23[:], ps_b[1][:])
         for u in range(2):
             nc.vector.tensor_copy(pv[2 + u][:].indirect(l4[:]), b23[:, u, :])
 
@@ -149,36 +151,47 @@ def tile_list_twoboardsweighed_tied_store_plain_kernel(
         diff = tile([P, PACK, O], F32, "diff")
         for t in range(PACK):
             ua = tile([P, O], F32, f"ua{t}")
-            ub = tile([P, O], F32, f"ub{t}")
             nc.scalar.activation(ua[:], pw[t][:].indirect(l5[:]), ACT.Copy, scale=sa_sb[:, t : t + 1])
-            nc.scalar.activation(ub[:], pv[t][:].indirect(l6[:]), ACT.Copy, scale=sb_sb[:, t : t + 1])
-            nc.vector.tensor_tensor(diff[:, t, :], ua[:], ub[:], ALU.subtract)
-
-        hq = tile([P, O], U32, "hq")
-        hs = tile([P, O], U8, "hs")
-        hid = tile([P, O, PACK], BF16, "hid")
-        d0 = diff[:, :, 0:SPLIT].rearrange("p t o -> p o t")
-        nc.vector.scalar_tensor_tensor(hid[:, 0:SPLIT, :], d0, -1.0, d0, ALU.mult, ALU.max)
-        nc.scalar.activation(
-            hid[:, SPLIT:O, :].rearrange("p (c i) t -> p c t i", i=4),
-            diff[:, :, SPLIT:O].rearrange("p t (c i) -> p c t i", i=4),
-            ACT.Abs,
-        )
-        nc.vector.quantize_mx(hq[:].bitcast(E5M2), hs[:], hid[:].rearrange("p o t -> p (o t)"))
-
-        for h in range(2):
-            rows = slice(P * h, P * (h + 1))
-            y = psum.tile([P, O], F32, name=f"ps_y{h}")
-            nc.tensor.matmul_mx(
-                y[:],
-                lhsT=vgw[:, rows].bitcast(E4M3), lhsT_scale=vgs[:, rows],
-                rhs=hq[:].bitcast(E5M2), rhs_scale=hs[:],
-                start=True, stop=True,
-            )
-            y_sb = tile([P, O], F32, f"y_sb{h}")
-            if h == 0:
-                nc.scalar.copy(y_sb[:], y[:])
-                nc.scalar.dma_start(out[rows, :], y_sb[:])
+            if t < PACK - 1:
+                ub = tile([P, O], F32, f"ub{t}")
+                nc.scalar.activation(ub[:], pv[t][:].indirect(l6[:]), ACT.Copy, scale=sb_sb[:, t : t + 1])
+                nc.vector.tensor_tensor(diff[:, t, :], ua[:], ub[:], ALU.subtract)
             else:
-                nc.vector.tensor_copy(y_sb[:], y[:])
-                nc.sync.dma_start(out[rows, :], y_sb[:])
+                for h in range(2):
+                    cols = slice(HALF * h, HALF * (h + 1))
+                    ub = tile([P, HALF], F32, f"ub{t}_{h}")
+                    nc.scalar.activation(ub[:], pv[t][:].indirect(l6[:, 8 * h : 8 * h + 8]), ACT.Copy, scale=sb_sb[:, t : t + 1])
+                    nc.vector.tensor_tensor(diff[:, t, cols], ua[:, cols], ub[:], ALU.subtract)
+
+        hid = [tile([P, HALF, PACK], BF16, f"hid{h}") for h in range(2)]
+        for dst, cols in ((hid[0][:], slice(0, HALF)), (hid[1][:, 0 : CUT - HALF, :], slice(HALF, CUT))):
+            nc.scalar.activation(
+                dst.rearrange("p (c i) t -> p c t i", i=4),
+                diff[:, :, cols].rearrange("p t (c i) -> p c t i", i=4),
+                ACT.Abs,
+            )
+        rest = diff[:, :, CUT:O].rearrange("p t o -> p o t")
+        nc.vector.scalar_tensor_tensor(hid[1][:, CUT - HALF : HALF, :], rest, -1.0, rest, ALU.mult, ALU.max)
+
+        y0 = psum.tile([P, 2, HALF], F32, name="ps_y0")
+        y1 = [psum.tile([P, HALF], F32, name=f"ps_y1{g}") for g in range(2)]
+        for h in range(2):
+            hq = tile([P, HALF], U32, f"hq{h}")
+            hs = tile([P, HALF], U8, f"hs{h}")
+            nc.vector.quantize_mx(hq[:].bitcast(E5M2), hs[:], hid[h][:].rearrange("p o t -> p (o t)"))
+            for g in range(2):
+                rows = slice(P * g, P * (g + 1))
+                nc.tensor.matmul_mx(
+                    y0[:, g, :] if h == 0 else y1[g][:],
+                    lhsT=vgw[:, rows].bitcast(E4M3), lhsT_scale=vgs[:, rows],
+                    rhs=hq[:].bitcast(E5M2), rhs_scale=hs[:],
+                    start=True, stop=True,
+                )
+        y0_sb = tile([P, 2, HALF], F32, "y0_sb")
+        nc.scalar.copy(y0_sb[:], y0[:])
+        nc.sync.dma_start(out[:, 0:HALF].rearrange("(g p) o -> p g o", p=P), y0_sb[:])
+        y1_sb = [tile([P, HALF], F32, f"y1_sb{g}") for g in range(2)]
+        nc.scalar.copy(y1_sb[0][:], y1[0][:])
+        nc.scalar.dma_start(out[0:P, HALF:O], y1_sb[0][:])
+        nc.vector.tensor_copy(y1_sb[1][:], y1[1][:])
+        nc.sync.dma_start(out[P : 2 * P, HALF:O], y1_sb[1][:])

from contextlib import ExitStack

import concourse.mybir as mybir

K, T, J, R, C, O, N, S = 512, 2048, 256, 512, 512, 256, 256, 1024
FLOPS = 2 * (2 * K * R * J + R * N * O)

F32 = mybir.dt.float32
BF16 = mybir.dt.bfloat16
I32 = mybir.dt.int32
U32 = mybir.dt.uint32
U16 = mybir.dt.uint16
U8 = mybir.dt.uint8
E2M1 = mybir.dt.float4_e2m1fn_x4
E5M2 = mybir.dt.float8_e5m2_x4
E4M3 = mybir.dt.float8_e4m3fn_x4
ALU = mybir.AluOpType
ACT = mybir.ActivationFunctionType

P = 128
PACK = 4
QUADS = 4
QROWS = 4
HALF = O // 2
CUT = 168


def tile_list_twoboardsweighed_tied_store_plain_kernel(
    tc, xt_words, xt_scales, w_words, w_scales, sa, sb, vs_words, vs_scales,
    offs, offs2, offs3, offs4, offs5, offs6, offs7, out,
):
    nc = tc.nc
    with ExitStack() as ctx:
        keep = ctx.enter_context(tc.tile_pool(name="keep", bufs=1))
        psum = ctx.enter_context(tc.psum_pool(name="psum", bufs=1))

        def tile(shape, dtype, name, tag=None):
            return keep.tile(shape, dtype, name=name, tag=tag or name, align_bytes=64)

        def load_list(src, name):
            dst = tile([P, J // 16], U16, name)
            nc.sync.dma_start(dst[:], src)
            return dst

        def load_plane(dst, src):
            for q in range(QUADS):
                nc.sync.dma_start(
                    dst[32 * q : 32 * q + QROWS, :].bitcast(I32),
                    src[0, QROWS * q : QROWS * (q + 1), :].bitcast(I32),
                )

        xs = tile([P, T], U8, "xs")
        ws = tile([P, R], U8, "ws")
        vsc = tile([P, S], U8, "vsc")
        nc.vector.memset(xs[:].bitcast(I32), 0)
        nc.vector.memset(ws[:].bitcast(I32), 0)
        pw = [tile([P, C], F32, f"pw{t}") for t in range(2)]
        for t in range(2):
            nc.vector.memset(pw[t][:], 0.0)
        nc.vector.memset(vsc[:].bitcast(I32), 0)

        l1 = load_list(offs, "l1")
        xw = tile([P, T], U16, "xw")
        nc.sync.dma_start(xw[:].bitcast(I32), xt_words[0].bitcast(I32))
        ws_rows = tile([QROWS, QUADS, R // 4], I32, "ws_rows")
        nc.scalar.dma_start(ws_rows[:], w_scales[0].bitcast(I32).rearrange("(q r) c -> r q c", r=QROWS))
        load_plane(xs, xt_scales)
        ww = tile([P, R], U32, "ww")
        nc.sync.dma_start(ww[:].bitcast(I32), w_words[0].rearrange("p c b -> p (c b)").bitcast(I32))
        l2 = load_list(offs2, "l2")
        l3 = load_list(offs3, "l3")
        l7 = load_list(offs7, "l7")
        vw = tile([P, S], U32, "vw")
        nc.sync.dma_start(vw[:].bitcast(I32), vs_words[0].rearrange("p c b -> p (c b)").bitcast(I32))
        load_plane(vsc, vs_scales)
        l4 = load_list(offs4, "l4")
        l5 = load_list(offs5, "l5")
        l6 = load_list(offs6, "l6")
        sa_sb = tile([P, PACK], F32, "sa_sb")
        sb_sb = tile([P, PACK], F32, "sb_sb")
        nc.sync.dma_start(sa_sb[:], sa.rearrange("(p t) one -> p (t one)", t=PACK))
        nc.sync.dma_start(sb_sb[:], sb.rearrange("(p t) one -> p (t one)", t=PACK))

        for q in range(QUADS):
            nc.vector.tensor_copy(ws[32 * q : 32 * q + QROWS, :].bitcast(I32), ws_rows[:, q, :])
        wsp = tile([P, R], U8, "wsp")
        nc.vector.tensor_copy(
            wsp[:].rearrange("p (t c i) -> p c t i", t=PACK, i=16),
            ws[:].rearrange("p (c i t) -> p c t i", t=PACK, i=16),
        )
        wwp = tile([P, R], U32, "wwp")
        for t0 in (0, 2):
            nc.scalar.copy(
                wwp[:].rearrange("p (t c i) -> p c t i", t=PACK, i=4)[:, :, t0 : t0 + 2, :],
                ww[:].rearrange("p (c i t) -> p c t i", t=PACK, i=4)[:, :, t0 : t0 + 2, :],
            )

        def first_stage(name, lst, groups):
            gw = tile([P, J], U16, f"gw_{name}")
            gs = tile([P, J], U8, f"gs_{name}")
            nc.vector.tensor_copy(gw[:], xw[:].indirect(lst[:]))
            nc.vector.tensor_copy(gs[:], xs[:].indirect(lst[:]))
            banks = []
            for group in groups:
                bank = psum.tile([P, len(group), J], F32, name=f"ps_{name}{group[0]}")
                for u, t in enumerate(group):
                    cols = slice(P * t, P * (t + 1))
                    nc.tensor.matmul_mx(
                        bank[:, u, :],
                        lhsT=wwp[:, cols].bitcast(E5M2), lhsT_scale=wsp[:, cols],
                        rhs=gw[:].bitcast(E2M1), rhs_scale=gs[:],
                        start=True, stop=True,
                    )
                banks.append(bank)
            return banks

        ps_a = first_stage("a", l1, ((0,), (1,), (2, 3)))
        ps_b = first_stage("b", l2, ((0, 1), (2, 3)))

        def late_page(name, tag):
            page = tile([P, C], F32, name, tag)
            nc.gpsimd.memset(page[:], 0.0)
            return page

        pw.extend([late_page("pw2", "ws"), late_page("pw3", "ww")])
        pv = [late_page(f"pv{t}", tag) for t, tag in enumerate(("xw", "xs", "gw_a", "gs_a"))]

        a0 = tile([P, 1, J], F32, "a0")
        a1 = tile([P, 1, J], F32, "a1")
        a23 = tile([P, 2, J], F32, "a23")
        b01 = tile([P, 2, J], F32, "b01")
        b23 = tile([P, 2, J], F32, "b23")
        nc.scalar.copy(a0[:], ps_a[0][:])
        nc.scalar.copy(a1[:], ps_a[1][:])
        nc.vector.tensor_copy(pw[0][:].indirect(l3[:]), a0[:, 0, :])
        nc.scalar.activation(pw[1][:].indirect(l3[:]), a1[:, 0, :], ACT.Copy)
        nc.vector.tensor_copy(a23[:], ps_a[2][:])
        nc.scalar.copy(b01[:], ps_b[0][:])
        for u in range(2):
            nc.vector.tensor_copy(pw[2 + u][:].indirect(l3[:]), a23[:, u, :])
            nc.scalar.activation(pv[u][:].indirect(l4[:]), b01[:, u, :], ACT.Copy)
        nc.vector.tensor_copy(b23[:], ps_b[1][:])
        for u in range(2):
            nc.vector.tensor_copy(pv[2 + u][:].indirect(l4[:]), b23[:, u, :])

        vgs = tile([P, N], U8, "vgs")
        vgw = tile([P, N], U32, "vgw")
        nc.vector.tensor_copy(vgw[:], vw[:].indirect(l7[:]))
        nc.vector.tensor_copy(vgs[:], vsc[:].indirect(l7[:]))

        diff = tile([P, PACK, O], F32, "diff")
        for t in range(PACK):
            ua = tile([P, O], F32, f"ua{t}")
            nc.scalar.activation(ua[:], pw[t][:].indirect(l5[:]), ACT.Copy, scale=sa_sb[:, t : t + 1])
            if t < PACK - 1:
                ub = tile([P, O], F32, f"ub{t}")
                nc.scalar.activation(ub[:], pv[t][:].indirect(l6[:]), ACT.Copy, scale=sb_sb[:, t : t + 1])
                nc.vector.tensor_tensor(diff[:, t, :], ua[:], ub[:], ALU.subtract)
            else:
                for h in range(2):
                    cols = slice(HALF * h, HALF * (h + 1))
                    ub = tile([P, HALF], F32, f"ub{t}_{h}")
                    nc.scalar.activation(ub[:], pv[t][:].indirect(l6[:, 8 * h : 8 * h + 8]), ACT.Copy, scale=sb_sb[:, t : t + 1])
                    nc.vector.tensor_tensor(diff[:, t, cols], ua[:, cols], ub[:], ALU.subtract)

        hid = [tile([P, HALF, PACK], BF16, f"hid{h}") for h in range(2)]
        for dst, cols in ((hid[0][:], slice(0, HALF)), (hid[1][:, 0 : CUT - HALF, :], slice(HALF, CUT))):
            nc.scalar.activation(
                dst.rearrange("p (c i) t -> p c t i", i=4),
                diff[:, :, cols].rearrange("p t (c i) -> p c t i", i=4),
                ACT.Abs,
            )
        rest = diff[:, :, CUT:O].rearrange("p t o -> p o t")
        nc.vector.scalar_tensor_tensor(hid[1][:, CUT - HALF : HALF, :], rest, -1.0, rest, ALU.mult, ALU.max)

        y0 = psum.tile([P, 2, HALF], F32, name="ps_y0")
        y1 = [psum.tile([P, HALF], F32, name=f"ps_y1{g}") for g in range(2)]
        for h in range(2):
            hq = tile([P, HALF], U32, f"hq{h}")
            hs = tile([P, HALF], U8, f"hs{h}")
            nc.vector.quantize_mx(hq[:].bitcast(E5M2), hs[:], hid[h][:].rearrange("p o t -> p (o t)"))
            for g in range(2):
                rows = slice(P * g, P * (g + 1))
                nc.tensor.matmul_mx(
                    y0[:, g, :] if h == 0 else y1[g][:],
                    lhsT=vgw[:, rows].bitcast(E4M3), lhsT_scale=vgs[:, rows],
                    rhs=hq[:].bitcast(E5M2), rhs_scale=hs[:],
                    start=True, stop=True,
                )
        y0_sb = tile([P, 2, HALF], F32, "y0_sb")
        nc.scalar.copy(y0_sb[:], y0[:])
        nc.sync.dma_start(out[:, 0:HALF].rearrange("(g p) o -> p g o", p=P), y0_sb[:])
        y1_sb = [tile([P, HALF], F32, f"y1_sb{g}") for g in range(2)]
        nc.scalar.copy(y1_sb[0][:], y1[0][:])
        nc.scalar.dma_start(out[0:P, HALF:O], y1_sb[0][:])
        nc.vector.tensor_copy(y1_sb[1][:], y1[1][:])
        nc.sync.dma_start(out[P : 2 * P, HALF:O], y1_sb[1][:])
